import numpy as np
import ml_dtypes


def mxq(x, axis, fmt="e4m3"):
    dtype, down = {"e4m3": (ml_dtypes.float8_e4m3fn, 7), "e5m2": (ml_dtypes.float8_e5m2, 14)}[fmt]
    v = np.moveaxis(np.asarray(x, np.float32).astype(ml_dtypes.bfloat16).astype(np.float64), axis, -1)
    blocks = v.reshape(v.shape[:-1] + (-1, 32))
    amax = np.abs(blocks).max(-1, keepdims=True)
    byte = np.maximum(np.where(amax > 0, np.frexp(amax)[1] - 1 + 127, 0) - down, 1)
    scale = np.exp2(byte - 127.0)
    codes = (blocks / scale).astype(np.float32).astype(dtype).astype(np.float64)
    return np.moveaxis((codes * scale).reshape(v.shape), -1, axis)


WIDE = False


def mx_kscale(k):
    if not WIDE:
        return np.ones(k)
    levels = np.array([10, -10, 5, -5, 0])
    if k % 512:
        return np.exp2(np.random.permutation(np.resize(levels, k // 32))).repeat(32)
    a = np.empty((k // 512, 16))
    for p in range(k // 512):
        a[p, :8] = np.random.permutation(np.resize(levels, 8))
        for g in range(8):
            far = levels[np.abs(levels - a[p, g]) >= 10]
            a[p, g + 8] = far[np.random.randint(len(far))]
    return np.exp2(a.ravel()).repeat(32)


BF16 = ml_dtypes.bfloat16


def bf(x):
    return np.asarray(x, np.float32).astype(BF16)


def f64(x):
    return np.asarray(x).astype(np.float64)


B, V, H = 2048, 1024, 512


def draw0():
    c = mx_kscale(H)
    t = mx_kscale(B)
    u = mx_kscale(B)
    return {"v": bf(np.random.uniform(-1.0, 1.0, (B, V)) * u[:, None]),
            "hp": bf(np.random.uniform(-1.0, 1.0, (B, H)) / u[:, None]),
            "hf": bf(np.random.uniform(-1.0, 1.0, (B, H)) * c),
            "hn": bf(np.random.uniform(-1.0, 1.0, (B, H)) / t[:, None]),
            "w": bf(np.random.standard_normal((V, H)) * 2.0 / np.sqrt(H) / c),
            "b": bf(0.3 * np.random.standard_normal(V)),
            "s": bf((1.0 + 0.1 * np.random.standard_normal(B)) * t)}


def visible_mean_field(h, w, b):
    return np.tanh((mxq(h, 1, "e4m3") @ mxq(w, 1, "e4m3").T) + b)


def correlation(vis, hid):
    return mxq(vis, 0, "e4m3").T @ mxq(hid, 0, "e4m3")


def core(v, hp, hf, hn, w, b, s):
    n_rows = v.shape[0]
    v1 = visible_mean_field(f64(hf), f64(w), f64(b))
    v1s = f64(s)[:, None] * v1
    neg = correlation(v1s, f64(hn))
    pos = correlation(f64(v), f64(hp))
    g = (pos - neg) / np.sqrt(n_rows)
    return g


def e4m3fn_bytes(y):
    return np.clip(np.asarray(y, np.float64), -448.0, 448.0).astype(np.float32).astype(ml_dtypes.float8_e4m3fn).view(np.uint8)


def e4m3fn_values(b):
    return np.asarray(b, np.uint8).view(ml_dtypes.float8_e4m3fn).astype(np.float64)


def setup_inputs():
    d = draw0()
    x0 = np.asarray(d['v']).astype(np.float64)
    s = (np.max(np.abs(x0), axis=(1,), keepdims=True) / 448.0).astype(np.float32)
    out = {}
    for k, v in d.items():
        if k == 'v':
            out['v_bytes'] = e4m3fn_bytes(x0 / s.astype(np.float64))
            out['v_scale'] = s
        else:
            out[k] = v
    return out


def reference(v_bytes, v_scale, hp, hf, hn, w, b, s):
    return core(e4m3fn_values(v_bytes) * v_scale.astype(np.float64), hp, hf, hn, w, b, s)

from contextlib import ExitStack

import concourse.mybir as mybir
from concourse.masks import make_identity

ROWS, VIS, HID = 2048, 1024, 512
FLOPS = 3 * 2 * ROWS * VIS * HID

F32 = mybir.dt.float32
BF16 = mybir.dt.bfloat16
U32 = mybir.dt.uint32
U8 = mybir.dt.uint8
FP8 = mybir.dt.float8_e4m3fn
FP8X4 = mybir.dt.float8_e4m3fn_x4
ACT = mybir.ActivationFunctionType
ALU = mybir.AluOpType

P = 128
T = 4
G = ROWS // (P * T)
M = VIS // P


def tile_persistentmeanfieldisingrbmgradient_kernel(tc, v_bytes, v_scale, hp, hf, hn, w, b, s, out):
    nc = tc.nc
    with ExitStack() as ctx:
        keep = ctx.enter_context(tc.tile_pool(name="keep", bufs=1))
        stage = ctx.enter_context(tc.tile_pool(name="stage", bufs=3))
        psum = ctx.enter_context(tc.psum_pool(name="psum", bufs=1))

        warm = keep.tile([P, 1], F32, name="warm")
        nc.vector.memset(warm[:], 0.0)
        warm_out = keep.tile([P, 1], F32, name="warm_out")
        nc.scalar.activation(out=warm_out[:], in_=warm[:], func=ACT.Tanh)
        ident = keep.tile([P, P], F32, name="ident")
        make_identity(nc, ident[:])
        b_rows = keep.tile([P, P], BF16, name="b_rows")
        nc.vector.memset(b_rows[:], 0.0)
        nc.scalar.dma_start(out=b_rows[0:M, :], in_=b.rearrange("(m p) -> m p", p=P))
        s_bf = keep.tile([P, G, T], BF16, name="s_bf")
        nc.scalar.dma_start(out=s_bf[:], in_=s.rearrange("(g p t) -> p g t", p=P, t=T))
        v_sc = keep.tile([P, G, T], F32, name="v_sc")
        nc.scalar.dma_start(out=v_sc[:], in_=v_scale.rearrange("(g p t) o -> p g (t o)", p=P, t=T))

        rows4 = {}

        def load_rows(key, src, g):
            dst = keep.tile([P, T * HID], BF16, name="%s_raw%d" % (key, g), align_bytes=64)
            nc.sync.dma_start(out=dst[:], in_=src.rearrange("(g p t) k -> g p (t k)", p=P, t=T)[g])
            rows4[key, g] = dst

        w_raw = keep.tile([P, M, HID], BF16, name="w_raw", align_bytes=64)
        w_view = w.rearrange("(m p) k -> p m k", p=P)
        v_raw = {}

        def load_v(g):
            dst = keep.tile([P, T * VIS], U8, name="v_codes_in%d" % g, align_bytes=64)
            nc.sync.dma_start(out=dst[:], in_=v_bytes.rearrange("(g p t) c -> g p (t c)", p=P, t=T)[g])
            v_raw[g] = dst

        load_rows("hn", hn, 0)
        load_v(0)
        nc.sync.dma_start(out=w_raw[:, 0:2, :], in_=w_view[:, 0:2, :])
        load_rows("hf", hf, 0)
        load_rows("hn", hn, 1)
        load_rows("hf", hf, 1)
        load_rows("hf", hf, 2)
        load_v(1)
        load_rows("hf", hf, 3)
        load_rows("hn", hn, 2)
        load_rows("hn", hn, 3)
        load_rows("hp", hp, 0)
        nc.sync.dma_start(out=w_raw[:, 2:8, :], in_=w_view[:, 2:8, :])
        load_rows("hp", hp, 1)
        load_v(2)
        load_rows("hp", hp, 2)
        load_v(3)
        load_rows("hp", hp, 3)

        b_sq = keep.tile([P, P], F32, name="b_sq")
        nc.vector.tensor_copy(out=b_sq[:], in_=b_rows[:])
        s_neg = keep.tile([P, G, T], F32, name="s_neg")
        nc.vector.tensor_scalar(out=s_neg[:], in0=s_bf[:], scalar1=-1.0, scalar2=None, op0=ALU.mult)
        b_turn = psum.tile([P, 2, 2, P], F32, name="b_turn", tag="turn", bufs=3)
        nc.tensor.transpose(b_turn[:, 0, 0, :], b_sq[:], ident[:])
        b_col = keep.tile([P, M], F32, name="b_col")
        nc.scalar.copy(out=b_col[:], in_=b_turn[:, 0, 0, 0:M])

        codes = {}
        grouped_of = {}

        def quantize(key, grouped):
            width = grouped.shape[1] // T
            c = keep.tile([P, width], U32, name="c_" + "_".join([str(k) for k in key]), align_bytes=64)
            sc = keep.tile([P, width], U8, name="s_" + "_".join([str(k) for k in key]), align_bytes=64)
            nc.vector.quantize_mx(out=c[:].bitcast(FP8X4), scales=sc[:], in_=grouped)
            codes[key] = (c, sc)

        def turn_pair(words, grouped):
            xt = psum.tile([P, 2, 2, P], F32, name="xt", tag="turn", bufs=3)
            for i in range(2):
                for u in range(2):
                    nc.tensor.transpose(xt[:, i, u, :], words[:, 256 * i + u : 256 * (i + 1) : 2], ident[:])
            nc.scalar.copy(
                out=grouped.bitcast(F32).rearrange("p (i r u) -> p i r u", i=2, u=2),
                in_=xt[:].rearrange("p i u r -> p i r u"),
            )

        def turn_w(pair):
            grouped = stage.tile([P, 1024], BF16, name="w_grouped", align_bytes=64, bufs=2)
            words = w_raw[:, 2 * pair : 2 * pair + 2, :].rearrange("p m k -> p (m k)").bitcast(F32)
            turn_pair(words, grouped[:])
            grouped_of["w", pair] = grouped

        def turn_hf(g):
            grouped = stage.tile([P, 2048], BF16, name="hf_grouped", align_bytes=64, bufs=2)
            words = rows4["hf", g][:].bitcast(F32)
            for h in range(2):
                turn_pair(words[:, 512 * h : 512 * (h + 1)], grouped[:, 1024 * h : 1024 * (h + 1)])
            grouped_of["hf", g] = grouped

        def q_grouped(key):
            quantize(key, grouped_of[key][:])

        def interleave(key, g, on_scalar=False):
            grouped = stage.tile([P, 2048], BF16, name="h_grouped", align_bytes=64, bufs=3)
            dst = grouped[:].rearrange("p (c i t) -> p c t i", i=4, t=T)
            src = rows4[key, g][:].rearrange("p (t c i) -> p c t i", t=T, i=4)
            if on_scalar:
                nc.scalar.copy(out=dst, in_=src)
            else:
                nc.vector.tensor_copy(out=dst, in_=src)
            grouped_of[key, g] = grouped

        wide_of = {}

        def widen(half, g):
            wide = stage.tile([P, T, 512], BF16, name="wide", align_bytes=64, bufs=8)
            for t in range(T):
                lo = VIS * t + 512 * half
                nc.scalar.activation(
                    out=wide[:, t, :],
                    in_=v_raw[g][:, lo : lo + 512].bitcast(FP8),
                    func=ACT.Copy,
                    scale=v_sc[:, g, t : t + 1],
                )
            wide_of[half, g] = wide

        def inter_v(chunk, g):
            grouped = stage.tile([P, 1024], BF16, name="v_grouped", align_bytes=64, bufs=3)
            lo = 256 * (chunk % 2)
            dst = grouped[:].rearrange("p (c i t) -> p c t i", i=4, t=T)
            src = wide_of[chunk // 2, g][:, :, lo : lo + 256].rearrange("p t (c i) -> p c t i", i=4)
            nc.vector.tensor_copy(out=dst, in_=src)
            grouped_of["v", chunk, g] = grouped

        def mx(dst, lhs, l0, rhs, start, stop):
            lc, ls = codes[lhs]
            rc, rs = codes[rhs]
            nc.tensor.matmul_mx(
                out=dst,
                lhsT=lc[:, l0 : l0 + P].bitcast(FP8X4),
                lhsT_scale=ls[:, l0 : l0 + P],
                rhs=rc[:].bitcast(FP8X4),
                rhs_scale=rs[:],
                start=start,
                stop=stop,
            )

        fields = {}
        z_of = {}

        def field(j):
            m, g = divmod(j, G)
            z = psum.tile([P, 512], F32, name="z", tag="z", bufs=2)
            mx(z[:], ("w", m // 2), P * (m % 2), ("hf", g), True, True)
            z_of[j] = z

        def tanh(j):
            m = j // G
            z = z_of[j]
            th = stage.tile([P, 512], F32, name="th", bufs=6)
            nc.scalar.activation(out=th[:], in_=z[:], func=ACT.Tanh, bias=b_col[:, m : m + 1])
            fields[j] = th

        turned = {}

        def turn_field(j):
            xt = psum.tile([P, T, P], F32, name="xf", tag="turn", bufs=3)
            for t in range(T):
                nc.tensor.transpose(xt[:, t, :], fields[j][:, P * t : P * (t + 1)], ident[:])
            turned[j] = xt

        v1g = {}

        def weigh(j):
            g = j % G
            if j % 2 == 0:
                grouped = stage.tile([P, 1024], BF16, name="v1_grouped", align_bytes=64, bufs=3)
                v1g[j // 2] = grouped
            dst = v1g[j // 2][:, 512 * (j % 2) : 512 * (j % 2) + 512]
            nc.vector.tensor_tensor(
                out=dst.rearrange("p (c t) -> p c t", t=T),
                in0=turned[j][:].rearrange("p t c -> p c t"),
                in1=s_neg[:, g, :].unsqueeze(1).to_broadcast([P, P, T]),
                op=ALU.mult,
            )

        def q_v1(step):
            quantize(("v1", step), v1g[step][:])

        acc = {}
        ready = []
        done = {}

        def accumulate(m, lhs, l0, rhs):
            if m not in acc:
                a = psum.tile([P, HID], F32, name="acc", tag="acc", bufs=3)
                acc[m] = a
                done[m] = 0
            mx(acc[m][:], lhs, l0, rhs, done[m] == 0, done[m] == 2 * G - 1)
            done[m] += 1
            if done[m] == 2 * G:
                ready.append(m)

        def store_ready():
            for m in ready:
                res = stage.tile([P, HID], F32, name="res", bufs=3)
                nc.scalar.mul(out=res[:], in_=acc[m][:], mul=1.0 / (float(ROWS) ** 0.5))
                nc.sync.dma_start(out=out[P * m : P * (m + 1), :], in_=res[:])
            ready.clear()

        def neg(step):
            for j in (2 * step, 2 * step + 1):
                m, g = divmod(j, G)
                accumulate(m, ("v1", step), P * (j % 2), ("hn", g))

        def pos(m):
            for g in range(G):
                accumulate(m, ("v", m // 2, g), P * (m % 2), ("hp", g))

        prep = [("hn", g, False) for g in range(1, 4)] + [("hp", g, g in (1,)) for g in range(4)]
        prep = prep + [("v", c, g) for c in range(4) for g in range(G)]
        widened = set()
        progress = [0.0, 0, 0]
        pending_q = []

        def need_wide(k):
            for item in prep[k : k + 6]:
                if item[0] == "v":
                    key = (item[1] // 2, item[2])
                    if key not in widened:
                        widened.add(key)
                        widen(key[0], key[1])

        def prepare(limit):
            while progress[1] < len(prep) and progress[0] < limit:
                need_wide(progress[1])
                item = prep[progress[1]]
                if item[0] == "v":
                    inter_v(item[1], item[2])
                    progress[0] += 0.82
                else:
                    interleave(item[0], item[1], item[2])
                    progress[0] += 0.5 if item[2] else 1.55
                while pending_q:
                    q_grouped(pending_q.pop())
                pending_q.append(item if item[0] == "v" else item[0:2])
                progress[1] += 1
            if progress[1] == len(prep):
                while pending_q:
                    q_grouped(pending_q.pop())
            while progress[2] < M and ("v", progress[2] // 2, 3) in codes:
                pos(progress[2])
                progress[2] += 1

        interleave("hn", 0)
        widened.add((0, 0))
        turn_w(0)
        turn_hf(0)
        widen(0, 0)
        q_grouped(("w", 0))
        q_grouped(("hn", 0))
        q_grouped(("hf", 0))
        field(0)
        tanh(0)
        turn_hf(1)
        q_grouped(("hf", 1))
        field(1)
        tanh(1)
        turn_hf(2)
        q_grouped(("hf", 2))
        field(2)
        tanh(2)
        turn_hf(3)
        q_grouped(("hf", 3))
        prepare(3)
        for j in range(32):
            if j % 8 == 3 and j < 24:
                turn_w(j // 8 + 1)
                q_grouped(("w", j // 8 + 1))
            if j + 3 < 32:
                field(j + 3)
                tanh(j + 3)
            turn_field(j)
            weigh(j)
            if j % 2 == 1:
                q_v1(j // 2)
                if j >= 3:
                    neg(j // 2 - 1)
                store_ready()
            prepare(4 + 0.65 * j)
        neg(15)
        prepare(1000.0)
        store_ready()
